import numpy as np
import ml_dtypes


def mxq(x, axis, fmt="e4m3"):
    dtype, down = {"e4m3": (ml_dtypes.float8_e4m3fn, 7), "e5m2": (ml_dtypes.float8_e5m2, 14)}[fmt]
    v = np.moveaxis(np.asarray(x, np.float32).astype(ml_dtypes.bfloat16).astype(np.float64), axis, -1)
    blocks = v.reshape(v.shape[:-1] + (-1, 32))
    amax = np.abs(blocks).max(-1, keepdims=True)
    byte = np.maximum(np.where(amax > 0, np.frexp(amax)[1] - 1 + 127, 0) - down, 1)
    scale = np.exp2(byte - 127.0)
    codes = (blocks / scale).astype(np.float32).astype(dtype).astype(np.float64)
    return np.moveaxis((codes * scale).reshape(v.shape), -1, axis)


WIDE = False


def mx_kscale(k):
    if not WIDE:
        return np.ones(k)
    levels = np.array([10, -10, 5, -5, 0])
    if k % 512:
        return np.exp2(np.random.permutation(np.resize(levels, k // 32))).repeat(32)
    a = np.empty((k // 512, 16))
    for p in range(k // 512):
        a[p, :8] = np.random.permutation(np.resize(levels, 8))
        for g in range(8):
            far = levels[np.abs(levels - a[p, g]) >= 10]
            a[p, g + 8] = far[np.random.randint(len(far))]
    return np.exp2(a.ravel()).repeat(32)


def f64(x):
    return np.asarray(x).astype(np.float64)


def striped(idx):
    return np.tile(idx.reshape(-1, 16).T, (8, 1)).astype(np.uint16)


def unstriped(offs):
    return offs[:16].T.reshape(-1).astype(np.int64)


def striped8(idx):
    return np.concatenate([x.reshape(-1, 16).T for x in idx]).astype(np.uint16)


def runs(offs, k):
    lists = np.stack([offs[16 * r : 16 * r + 16].T.reshape(-1) for r in range(8)]).astype(np.int64)
    return lists[np.arange(k) % 512 // 64]


def pack_weight(w):
    k, n = w.shape
    w = f64(np.asarray(w, np.float32).astype(ml_dtypes.bfloat16)).reshape(k // 32, 32, n)
    amax = np.abs(w).max(1)
    byte = np.clip(np.where(amax > 0, np.frexp(amax)[1] - 1 + 127 - 7, 1), 1, 254)
    scaled = (w * np.exp2(127.0 - byte)[:, None, :]).reshape(k, n).astype(np.float32)
    words = np.ascontiguousarray(scaled.reshape(k // 512, 128, 4, n).transpose(0, 1, 3, 2)).astype(ml_dtypes.float8_e4m3fn).view(np.uint8)
    return words, np.ascontiguousarray(byte.astype(np.uint8).reshape(k // 512, 16, n))


def unpack_weight(words, scales):
    g, p, n, _ = words.shape
    vals = np.ascontiguousarray(words).view(ml_dtypes.float8_e4m3fn).astype(np.float64) * np.repeat(np.exp2(scales.astype(np.float64) - 127.0), 8, axis=1)[..., None]
    return vals.transpose(0, 1, 3, 2).reshape(g * 512, n)


K, T, S, N, G, H, W = 512, 2048, 512, 512, 2048, 512, 256


def setup_inputs():
    n = np.random.standard_normal
    s = mx_kscale(K)[:, None]
    u = mx_kscale(S)
    packed_xT = pack_weight(n((K, T)) * s)
    packed_dT = pack_weight(n((K, G)) / s)
    perm = np.stack([np.random.permutation(S) for _ in range(8)])
    return {
        "x_words": packed_xT[0],
        "x_scales": packed_xT[1],
        "d_words": packed_dT[0],
        "d_scales": packed_dT[1],
        "gn": (np.random.uniform(0.5, 1.5, (H, 1)) * u[:, None]).astype(np.float32),
        "w1": (n((H, N)) / np.sqrt(H) / u[:, None]).astype(np.float32),
        "offs": striped(np.random.permutation(T)[:S]),
        "k1": striped8(np.random.randint(0, G, (8, H))),
        "n1": striped8(np.stack([np.random.permutation(S)[:W] for _ in range(8)])),
        "n2": striped8(np.stack([np.random.permutation(S)[:W] for _ in range(8)])),
        "n3": striped8(np.stack([np.random.permutation(S) for _ in range(8)])),
        "n4": striped8(perm[:, :W]),
        "n5": striped8(perm[:, W:]),
    }


def reference(x_words, x_scales, d_words, d_scales, gn, w1, offs, k1, n1, n2, n3, n4, n5):
    d_k1 = unpack_weight(d_words, d_scales)[np.arange(K)[:, None], runs(k1, K)]
    xq = unpack_weight(x_words, x_scales)[:, unstriped(offs)]
    h = 0.0625 * (d_k1.T @ xq)
    pa = h[np.arange(H)[:, None], runs(n2, H)]
    ds = h.copy()
    ds[np.arange(H)[:, None], runs(n1, H)] = pa
    z = f64(gn) * (ds - (0.5 * (ds[np.arange(H)[:, None], runs(n3, H)])))
    h2 = mxq(f64(w1), 0, "e4m3").T @ mxq(z, 0, "e4m3")
    pb = h2[np.arange(N)[:, None], runs(n5, N)]
    pa2 = h2[np.arange(N)[:, None], runs(n4, N)]
    rb = pb - (0.5 * pa2)
    ra = np.sqrt((pa2) ** 2 + (pb) ** 2 + 0.25)
    ds2 = np.zeros((N, S))
    ds2[np.arange(N)[:, None], runs(n4, N)] = ra
    out = ds2.copy()
    out[np.arange(N)[:, None], runs(n5, N)] = rb
    return out

@@ -1,0 +1,198 @@
+from contextlib import ExitStack
+
+import concourse.mybir as mybir
+
+F32 = mybir.dt.float32
+BF16 = mybir.dt.bfloat16
+I32 = mybir.dt.int32
+U32 = mybir.dt.uint32
+U16 = mybir.dt.uint16
+U8 = mybir.dt.uint8
+FP8X4 = mybir.dt.float8_e4m3fn_x4
+ACT = mybir.ActivationFunctionType
+ALU = mybir.AluOpType
+
+P = 128
+PACK = 4
+TABLE = 2048
+S = 512
+W = 256
+HALF = 256
+FLOPS = 2 * 2 * 512 * 512 * 512
+
+
+def tile_picked_pqlayksetpolar_none_p_kernel(tc, x_words, x_scales, d_words, d_scales, gn, w1, offs, k1, n1, n2, n3, n4, n5, out):
+    nc = tc.nc
+    with ExitStack() as ctx:
+        lists = ctx.enter_context(tc.tile_pool(name="lists", bufs=1))
+        keep = ctx.enter_context(tc.tile_pool(name="keep", bufs=1))
+        psum = ctx.enter_context(tc.psum_pool(name="psum", bufs=8))
+
+        def load_list(src, name):
+            tile = lists.tile([P, src.shape[1]], U16, name=name)
+            nc.sync.dma_start(tile[:], src)
+            return tile
+
+        def halves():
+            return [slice(u * HALF, (u + 1) * HALF) for u in range(S // HALF)]
+
+        def entries(tile, cols):
+            return tile[:, cols.start // 16 : cols.stop // 16]
+
+        d_bytes = keep.tile([P, TABLE], U8, name="d_bytes")
+        x_bytes = keep.tile([P, TABLE], U8, name="x_bytes")
+        nc.vector.memset(d_bytes[:].bitcast(I32), 0)
+        nc.vector.memset(x_bytes[:].bitcast(I32), 0)
+
+        k1_t = load_list(k1, "k1_t")
+        nc.scalar.dma_start(d_bytes[0:P:8, :].bitcast(I32), d_scales[0].bitcast(I32))
+        offs_t = load_list(offs, "offs_t")
+        nc.scalar.dma_start(x_bytes[0:P:8, :].bitcast(I32), x_scales[0].bitcast(I32))
+        n2_t = load_list(n2, "n2_t")
+        d_table = keep.tile([P, TABLE], U32, name="d_table")
+        nc.sync.dma_start(d_table[:].bitcast(I32), d_words[0].rearrange("p n t -> p (n t)").bitcast(I32))
+        n1_t = load_list(n1, "n1_t")
+        n3_t = load_list(n3, "n3_t")
+        n4_t = load_list(n4, "n4_t")
+        n5_t = load_list(n5, "n5_t")
+        x_table = keep.tile([P, TABLE], U32, name="x_table")
+        nc.sync.dma_start(x_table[:].bitcast(I32), x_words[0].rearrange("p n t -> p (n t)").bitcast(I32))
+        gain = keep.tile([P, PACK], F32, name="gain")
+        nc.gpsimd.dma_start(gain[:], gn.rearrange("(p t) o -> p (t o)", t=PACK))
+        w_raw = [keep.tile([P, PACK, HALF], F32, name="w_raw%d" % u) for u in range(2)]
+        for u, cols in enumerate(halves()):
+            nc.sync.dma_start(w_raw[u][:], w1.rearrange("(p j) c -> p j c", j=PACK)[:, :, cols])
+        sixteenth = keep.tile([P, 1], F32, name="sixteenth")
+        nc.vector.memset(sixteenth[:], 0.0625)
+        quarter = keep.tile([P, 1], F32, name="quarter")
+        nc.scalar.activation(quarter[:], sixteenth[:], ACT.Sqrt)
+
+        d_bytes_g = keep.tile([P, S], U8, name="d_bytes_g")
+        nc.vector.tensor_copy(d_bytes_g[:], d_bytes[:].indirect(k1_t[:]))
+        x_bytes_g = keep.tile([P, S], U8, name="x_bytes_g")
+        nc.vector.tensor_copy(x_bytes_g[:], x_bytes[:].indirect(offs_t[:]))
+        planes = keep.tile([P, 2 * S], U8, name="planes", align_bytes=64)
+        d_plane = planes[:, :S]
+        x_plane = planes[:, S:]
+        nc.vector.tensor_copy(
+            d_plane.rearrange("p (t c i) -> p c t i", t=PACK, i=16),
+            d_bytes_g[:].rearrange("p (c i t) -> p c t i", t=PACK, i=16),
+        )
+        nc.vector.tensor_copy(x_plane.bitcast(U32), x_bytes_g[:].bitcast(U32))
+        for s in range(1, 4):
+            nc.scalar.dma_start(planes[s:P:32, :].bitcast(I32), planes[8 * s : P : 32, :].bitcast(I32))
+
+        d_picked = keep.tile([P, S], U32, name="d_picked")
+        nc.vector.tensor_copy(d_picked[:], d_table[:].indirect(k1_t[:]))
+        d_codes = keep.tile([P, S], U32, name="d_codes", align_bytes=64)
+        nc.vector.tensor_copy(
+            d_codes[:].rearrange("p (t c i) -> p c t i", t=PACK, i=4),
+            d_picked[:].rearrange("p (c i t) -> p c t i", t=PACK, i=4),
+        )
+        x_codes = [keep.tile([P, HALF], U32, name="x_codes%d" % u, align_bytes=64) for u in range(2)]
+        for u, cols in enumerate(halves()):
+            nc.vector.tensor_copy(x_codes[u][:], x_table[:].indirect(entries(offs_t, cols)))
+
+        gain16 = keep.tile([P, PACK], F32, name="gain16")
+        nc.scalar.activation(gain16[:], gain[:], ACT.Copy, scale=0.0625)
+
+        halves_of_s = halves()
+
+        def product(codes, plane, t, moving, moving_plane):
+            rows = slice(t * P, (t + 1) * P)
+            acc = psum.tile([P, HALF], F32, name="acc")
+            nc.tensor.matmul_mx(
+                acc[:], lhsT=codes[:, rows].bitcast(FP8X4), lhsT_scale=plane[:, rows],
+                rhs=moving.bitcast(FP8X4), rhs_scale=moving_plane, start=True, stop=True,
+            )
+            return acc
+
+        ds = [keep.tile([P, S], F32, name="ds%d" % t) for t in range(PACK)]
+
+        def first_layer(t, u):
+            cols = halves_of_s[u]
+            acc = product(d_codes, d_plane, t, x_codes[u][:], x_plane[:, cols])
+            nc.scalar.activation(ds[t][:, cols], acc[:], ACT.Copy, scale=gain16[:, t : t + 1])
+
+        w_grouped = keep.tile([P, PACK * 512], BF16, name="w_grouped", align_bytes=64)
+        for u in range(2):
+            nc.vector.tensor_copy(
+                w_grouped[:].rearrange("p (t m j) -> p m t j", t=PACK, j=PACK)[:, u * 64 : (u + 1) * 64],
+                w_raw[u][:].rearrange("p j (m t) -> p m t j", t=PACK),
+            )
+
+        z_rows = keep.tile([P, PACK, S], BF16, name="z_rows")
+        pa = [keep.tile([P, W], F32, name="pa%d" % t) for t in range(PACK)]
+        for t in range(PACK):
+            first_layer(t, 0)
+            first_layer(t, 1)
+            nc.scalar.activation(pa[t][:], ds[t][:].indirect(n2_t[:]), ACT.Copy)
+            nc.vector.tensor_copy(ds[t][:].indirect(n1_t[:]), pa[t][:])
+
+        w_codes = keep.tile([P, 512], U32, name="w_codes", align_bytes=64)
+        w_plane = keep.tile([P, 512], U8, name="w_plane", align_bytes=64)
+        nc.vector.quantize_mx(w_codes[:].bitcast(FP8X4), w_plane[:], w_grouped[:])
+
+        for t in range(PACK):
+            for cols in halves_of_s:
+                far = keep.tile([P, HALF], F32, name="far", bufs=8)
+                nc.scalar.activation(far[:], ds[t][:].indirect(entries(n3_t, cols)), ACT.Copy, scale=-0.5)
+                nc.vector.tensor_tensor(z_rows[:, t, cols], ds[t][:, cols], far[:], ALU.add)
+
+        h2 = [keep.tile([P, S], F32, name="h2_%d" % t) for t in range(PACK)]
+        z_codes = [keep.tile([P, HALF], U32, name="z_codes%d" % u, align_bytes=64) for u in range(2)]
+        z_plane = [keep.tile([P, HALF], U8, name="z_plane%d" % u, align_bytes=64) for u in range(2)]
+        z_grouped = [keep.tile([P, PACK * HALF], BF16, name="z_grouped%d" % u, align_bytes=64) for u in range(2)]
+        for u, cols in enumerate(halves_of_s):
+            nc.vector.tensor_copy(
+                z_grouped[u][:].rearrange("p (c i t) -> p c t i", t=PACK, i=4),
+                z_rows[:, :, cols].rearrange("p t (c i) -> p c t i", i=4),
+            )
+            nc.vector.quantize_mx(z_codes[u][:].bitcast(FP8X4), z_plane[u][:], z_grouped[u][:])
+
+        def second_layer(t, u):
+            acc = product(w_codes, w_plane, t, z_codes[u][:], z_plane[u][:])
+            nc.scalar.copy(h2[t][:, halves_of_s[u]], acc[:])
+
+        out_rows = out.rearrange("(p t) s -> p t s", t=PACK)
+        res = [keep.tile([P, S], F32, name="res%d" % t) for t in range(PACK)]
+        ra = [keep.tile([P, W], F32, name="ra%d" % t) for t in range(PACK)]
+        a_half = [keep.tile([P, W], F32, name="a_half%d" % t) for t in range(PACK)]
+        pb = [keep.tile([P, W], F32, name="pb%d" % t) for t in range(PACK)]
+
+        both = [keep.tile([P, W], F32, name="both%d" % t) for t in range(PACK)]
+
+        def fetch(t):
+            second_layer(t, 0)
+            second_layer(t, 1)
+            nc.scalar.activation(a_half[t][:], h2[t][:].indirect(n4_t[:]), ACT.Copy, scale=-0.5)
+            if t == 0:
+                nc.vector.tensor_copy(pb[t][:], h2[t][:].indirect(n5_t[:]))
+            else:
+                nc.scalar.activation(pb[t][:], h2[t][:].indirect(n5_t[:]), ACT.Copy)
+            nc.vector.tensor_tensor(res[t][:].indirect(n5_t[:]), pb[t][:], a_half[t][:], ALU.add)
+
+        def squares(t):
+            a_sq = keep.tile([P, W], F32, name="a_sq", bufs=4)
+            b_sq = keep.tile([P, W], F32, name="b_sq", bufs=4)
+            nc.scalar.activation(a_sq[:], a_half[t][:], ACT.Square, scale=2.0)
+            nc.scalar.activation(b_sq[:], pb[t][:], ACT.Square)
+            nc.vector.tensor_tensor(both[t][:], a_sq[:], b_sq[:], ALU.add)
+
+        def put_root(t):
+            nc.scalar.activation(ra[t][:], both[t][:], ACT.Sqrt, bias=quarter[:])
+            nc.vector.tensor_copy(res[t][:].indirect(n4_t[:]), ra[t][:])
+            nc.sync.dma_start(out_rows[:, t, :], res[t][:])
+
+        fetch(0)
+        fetch(1)
+        squares(0)
+        fetch(2)
+        put_root(0)
+        squares(1)
+        fetch(3)
+        put_root(1)
+        squares(2)
+        squares(3)
+        put_root(2)
+        put_root(3)

@@ -26,7 +26,7 @@ def tile_picked_pqlayksetpolar_none_p_kernel(tc, x_words, x_scales, d_words, d_s
     with ExitStack() as ctx:
         lists = ctx.enter_context(tc.tile_pool(name="lists", bufs=1))
         keep = ctx.enter_context(tc.tile_pool(name="keep", bufs=1))
-        psum = ctx.enter_context(tc.psum_pool(name="psum", bufs=8))
+        psum = ctx.enter_context(tc.psum_pool(name="psum", bufs=1))
 
         def load_list(src, name):
             tile = lists.tile([P, src.shape[1]], U16, name=name)
@@ -45,18 +45,18 @@ def tile_picked_pqlayksetpolar_none_p_kernel(tc, x_words, x_scales, d_words, d_s
         nc.vector.memset(x_bytes[:].bitcast(I32), 0)
 
         k1_t = load_list(k1, "k1_t")
-        nc.scalar.dma_start(d_bytes[0:P:8, :].bitcast(I32), d_scales[0].bitcast(I32))
+        nc.sync.dma_start(d_bytes[0:P:8, :].bitcast(I32), d_scales[0].bitcast(I32))
         offs_t = load_list(offs, "offs_t")
-        nc.scalar.dma_start(x_bytes[0:P:8, :].bitcast(I32), x_scales[0].bitcast(I32))
-        n2_t = load_list(n2, "n2_t")
+        nc.sync.dma_start(x_bytes[0:P:8, :].bitcast(I32), x_scales[0].bitcast(I32))
         d_table = keep.tile([P, TABLE], U32, name="d_table")
         nc.sync.dma_start(d_table[:].bitcast(I32), d_words[0].rearrange("p n t -> p (n t)").bitcast(I32))
+        n2_t = load_list(n2, "n2_t")
         n1_t = load_list(n1, "n1_t")
         n3_t = load_list(n3, "n3_t")
-        n4_t = load_list(n4, "n4_t")
-        n5_t = load_list(n5, "n5_t")
         x_table = keep.tile([P, TABLE], U32, name="x_table")
         nc.sync.dma_start(x_table[:].bitcast(I32), x_words[0].rearrange("p n t -> p (n t)").bitcast(I32))
+        n4_t = load_list(n4, "n4_t")
+        n5_t = load_list(n5, "n5_t")
         gain = keep.tile([P, PACK], F32, name="gain")
         nc.gpsimd.dma_start(gain[:], gn.rearrange("(p t) o -> p (t o)", t=PACK))
         w_raw = [keep.tile([P, PACK, HALF], F32, name="w_raw%d" % u) for u in range(2)]
@@ -89,18 +89,18 @@ def tile_picked_pqlayksetpolar_none_p_kernel(tc, x_words, x_scales, d_words, d_s
             d_codes[:].rearrange("p (t c i) -> p c t i", t=PACK, i=4),
             d_picked[:].rearrange("p (c i t) -> p c t i", t=PACK, i=4),
         )
-        x_codes = [keep.tile([P, HALF], U32, name="x_codes%d" % u, align_bytes=64) for u in range(2)]
-        for u, cols in enumerate(halves()):
-            nc.vector.tensor_copy(x_codes[u][:], x_table[:].indirect(entries(offs_t, cols)))
+        x_codes = keep.tile([P, S], U32, name="x_codes", align_bytes=64)
+        for cols in halves():
+            nc.vector.tensor_copy(x_codes[:, cols], x_table[:].indirect(entries(offs_t, cols)))
 
-        gain16 = keep.tile([P, PACK], F32, name="gain16")
+        gain16 = keep.tile([P, PACK], F32, name="gain16", tag="gain_then_far")
         nc.scalar.activation(gain16[:], gain[:], ACT.Copy, scale=0.0625)
 
         halves_of_s = halves()
 
-        def product(codes, plane, t, moving, moving_plane):
+        def product(codes, plane, t, moving, moving_plane, bank, bufs):
             rows = slice(t * P, (t + 1) * P)
-            acc = psum.tile([P, HALF], F32, name="acc")
+            acc = psum.tile([P, moving.shape[1]], F32, name="acc", tag=bank, bufs=bufs)
             nc.tensor.matmul_mx(
                 acc[:], lhsT=codes[:, rows].bitcast(FP8X4), lhsT_scale=plane[:, rows],
                 rhs=moving.bitcast(FP8X4), rhs_scale=moving_plane, start=True, stop=True,
@@ -109,66 +109,79 @@ def tile_picked_pqlayksetpolar_none_p_kernel(tc, x_words, x_scales, d_words, d_s
 
         ds = [keep.tile([P, S], F32, name="ds%d" % t) for t in range(PACK)]
 
-        def first_layer(t, u):
-            cols = halves_of_s[u]
-            acc = product(d_codes, d_plane, t, x_codes[u][:], x_plane[:, cols])
-            nc.scalar.activation(ds[t][:, cols], acc[:], ACT.Copy, scale=gain16[:, t : t + 1])
+        def first_layer(t):
+            for cols in halves_of_s if t == 0 else [slice(0, S)]:
+                acc = product(d_codes, d_plane, t, x_codes[:, cols], x_plane[:, cols], "first", 2)
+                nc.scalar.activation(ds[t][:, cols], acc[:], ACT.Copy, scale=gain16[:, t : t + 1])
+            nc.scalar.activation(pa[t][:], ds[t][:].indirect(n2_t[:]), ACT.Copy)
 
         w_grouped = keep.tile([P, PACK * 512], BF16, name="w_grouped", align_bytes=64)
-        for u in range(2):
-            nc.vector.tensor_copy(
+        for u, copy in enumerate((nc.vector.tensor_copy, nc.vector.tensor_copy)):
+            copy(
                 w_grouped[:].rearrange("p (t m j) -> p m t j", t=PACK, j=PACK)[:, u * 64 : (u + 1) * 64],
                 w_raw[u][:].rearrange("p j (m t) -> p m t j", t=PACK),
             )
-
-        z_rows = keep.tile([P, PACK, S], BF16, name="z_rows")
-        pa = [keep.tile([P, W], F32, name="pa%d" % t) for t in range(PACK)]
-        for t in range(PACK):
-            first_layer(t, 0)
-            first_layer(t, 1)
-            nc.scalar.activation(pa[t][:], ds[t][:].indirect(n2_t[:]), ACT.Copy)
-            nc.vector.tensor_copy(ds[t][:].indirect(n1_t[:]), pa[t][:])
 
         w_codes = keep.tile([P, 512], U32, name="w_codes", align_bytes=64)
         w_plane = keep.tile([P, 512], U8, name="w_plane", align_bytes=64)
         nc.vector.quantize_mx(w_codes[:].bitcast(FP8X4), w_plane[:], w_grouped[:])
 
+        z_rows = [keep.tile([P, PACK, HALF], BF16, name="z_rows%d" % u) for u in range(2)]
+        pa = [keep.tile([P, W], F32, name="pa%d" % t) for t in range(PACK)]
         for t in range(PACK):
-            for cols in halves_of_s:
-                far = keep.tile([P, HALF], F32, name="far", bufs=8)
-                nc.scalar.activation(far[:], ds[t][:].indirect(entries(n3_t, cols)), ACT.Copy, scale=-0.5)
-                nc.vector.tensor_tensor(z_rows[:, t, cols], ds[t][:, cols], far[:], ALU.add)
+            first_layer(t)
+            nc.vector.tensor_copy(ds[t][:].indirect(n1_t[:]), pa[t][:])
 
         h2 = [keep.tile([P, S], F32, name="h2_%d" % t) for t in range(PACK)]
-        z_codes = [keep.tile([P, HALF], U32, name="z_codes%d" % u, align_bytes=64) for u in range(2)]
-        z_plane = [keep.tile([P, HALF], U8, name="z_plane%d" % u, align_bytes=64) for u in range(2)]
+        z_codes = keep.tile([P, S], U32, name="z_codes", align_bytes=64)
+        z_plane = keep.tile([P, S], U8, name="z_plane", align_bytes=64)
         z_grouped = [keep.tile([P, PACK * HALF], BF16, name="z_grouped%d" % u, align_bytes=64) for u in range(2)]
-        for u, cols in enumerate(halves_of_s):
-            nc.vector.tensor_copy(
-                z_grouped[u][:].rearrange("p (c i t) -> p c t i", t=PACK, i=4),
-                z_rows[:, :, cols].rearrange("p t (c i) -> p c t i", i=4),
-            )
-            nc.vector.quantize_mx(z_codes[u][:].bitcast(FP8X4), z_plane[u][:], z_grouped[u][:])
+        far = keep.tile([P, PACK, S], F32, name="far", tag="gain_then_far")
 
-        def second_layer(t, u):
-            acc = product(w_codes, w_plane, t, z_codes[u][:], z_plane[u][:])
-            nc.scalar.copy(h2[t][:, halves_of_s[u]], acc[:])
+        def make_z(t, u):
+            cols = halves_of_s[u]
+            nc.scalar.activation(far[:, t, cols], ds[t][:].indirect(entries(n3_t, cols)), ACT.Copy, scale=-0.5)
+            nc.vector.tensor_tensor(z_rows[u][:, t, :], ds[t][:, cols], far[:, t, cols], ALU.add)
+
+        def group_z(u, copy):
+            copy(
+                z_grouped[u][:].rearrange("p (c i t) -> p c t i", t=PACK, i=4),
+                z_rows[u][:].rearrange("p t (c i) -> p c t i", i=4),
+            )
+
+        def quantize_z(u):
+            cols = halves_of_s[u]
+            nc.vector.quantize_mx(z_codes[:, cols].bitcast(FP8X4), z_plane[:, cols], z_grouped[u][:])
+
+        for t, u in ((0, 0), (1, 0), (0, 1), (2, 0), (1, 1), (3, 0), (2, 1), (3, 1)):
+            make_z(t, u)
+        group_z(0, nc.scalar.copy)
+        group_z(1, nc.vector.tensor_copy)
+        quantize_z(1)
+        quantize_z(0)
 
         out_rows = out.rearrange("(p t) s -> p t s", t=PACK)
         res = [keep.tile([P, S], F32, name="res%d" % t) for t in range(PACK)]
         ra = [keep.tile([P, W], F32, name="ra%d" % t) for t in range(PACK)]
         a_half = [keep.tile([P, W], F32, name="a_half%d" % t) for t in range(PACK)]
         pb = [keep.tile([P, W], F32, name="pb%d" % t) for t in range(PACK)]
-
         both = [keep.tile([P, W], F32, name="both%d" % t) for t in range(PACK)]
 
         def fetch(t):
-            second_layer(t, 0)
-            second_layer(t, 1)
-            nc.scalar.activation(a_half[t][:], h2[t][:].indirect(n4_t[:]), ACT.Copy, scale=-0.5)
             if t == 0:
+                low, high = halves_of_s
+                acc = product(w_codes, w_plane, t, z_codes[:, high], z_plane[:, high], "high", 1)
+                nc.scalar.copy(h2[t][:, high], acc[:])
+                acc = product(w_codes, w_plane, t, z_codes[:, low], z_plane[:, low], "low", 1)
+                nc.vector.tensor_copy(h2[t][:, low], acc[:])
+            else:
+                acc = product(w_codes, w_plane, t, z_codes[:], z_plane[:], "rows%d" % t, 1)
+                nc.scalar.copy(h2[t][:], acc[:])
+            if t == 0:
+                nc.vector.tensor_scalar(a_half[t][:], h2[t][:].indirect(n4_t[:]), -0.5, 0.0, ALU.mult, ALU.add)
                 nc.vector.tensor_copy(pb[t][:], h2[t][:].indirect(n5_t[:]))
             else:
+                nc.scalar.activation(a_half[t][:], h2[t][:].indirect(n4_t[:]), ACT.Copy, scale=-0.5)
                 nc.scalar.activation(pb[t][:], h2[t][:].indirect(n5_t[:]), ACT.Copy)
             nc.vector.tensor_tensor(res[t][:].indirect(n5_t[:]), pb[t][:], a_half[t][:], ALU.add)
 
@@ -191,8 +204,8 @@ def tile_picked_pqlayksetpolar_none_p_kernel(tc, x_words, x_scales, d_words, d_s
         put_root(0)
         squares(1)
         fetch(3)
-        put_root(1)
         squares(2)
+        put_root(1)
         squares(3)
         put_root(2)
         put_root(3)

@@ -1,6 +1,7 @@
 from contextlib import ExitStack
 
 import concourse.mybir as mybir
+from concourse.masks import make_identity
 
 F32 = mybir.dt.float32
 BF16 = mybir.dt.bfloat16
@@ -67,6 +68,9 @@ def tile_picked_pqlayksetpolar_none_p_kernel(tc, x_words, x_scales, d_words, d_s
         quarter = keep.tile([P, 1], F32, name="quarter")
         nc.scalar.activation(quarter[:], sixteenth[:], ACT.Sqrt)
 
+        ident = keep.tile([P, P], F32, name="ident")
+        make_identity(nc, ident[:])
+
         d_bytes_g = keep.tile([P, S], U8, name="d_bytes_g")
         nc.vector.tensor_copy(d_bytes_g[:], d_bytes[:].indirect(k1_t[:]))
         x_bytes_g = keep.tile([P, S], U8, name="x_bytes_g")
@@ -127,7 +131,7 @@ def tile_picked_pqlayksetpolar_none_p_kernel(tc, x_words, x_scales, d_words, d_s
         nc.vector.quantize_mx(w_codes[:].bitcast(FP8X4), w_plane[:], w_grouped[:])
 
         z_rows = [keep.tile([P, PACK, HALF], BF16, name="z_rows%d" % u) for u in range(2)]
-        pa = [keep.tile([P, W], F32, name="pa%d" % t) for t in range(PACK)]
+        pa = [keep.tile([P, W], F32, name="pa%d" % t, tag="pa%d" % t, align_bytes=64) for t in range(PACK)]
         for t in range(PACK):
             first_layer(t)
             nc.vector.tensor_copy(ds[t][:].indirect(n1_t[:]), pa[t][:])
@@ -165,7 +169,7 @@ def tile_picked_pqlayksetpolar_none_p_kernel(tc, x_words, x_scales, d_words, d_s
         ra = [keep.tile([P, W], F32, name="ra%d" % t) for t in range(PACK)]
         a_half = [keep.tile([P, W], F32, name="a_half%d" % t) for t in range(PACK)]
         pb = [keep.tile([P, W], F32, name="pb%d" % t) for t in range(PACK)]
-        both = [keep.tile([P, W], F32, name="both%d" % t) for t in range(PACK)]
+        both = {}
 
         def fetch(t):
             if t == 0:
@@ -186,11 +190,20 @@ def tile_picked_pqlayksetpolar_none_p_kernel(tc, x_words, x_scales, d_words, d_s
             nc.vector.tensor_tensor(res[t][:].indirect(n5_t[:]), pb[t][:], a_half[t][:], ALU.add)
 
         def squares(t):
-            a_sq = keep.tile([P, W], F32, name="a_sq", bufs=4)
-            b_sq = keep.tile([P, W], F32, name="b_sq", bufs=4)
-            nc.scalar.activation(a_sq[:], a_half[t][:], ACT.Square, scale=2.0)
-            nc.scalar.activation(b_sq[:], pb[t][:], ACT.Square)
-            nc.vector.tensor_tensor(both[t][:], a_sq[:], b_sq[:], ALU.add)
+            turned = psum.tile([P, 2 * W], F32, name="turned", tag="first", bufs=2)
+            for n, src in enumerate((a_half[t], pb[t])):
+                for b in range(W // P):
+                    nc.tensor.transpose(turned[:, n * W + b * P : n * W + (b + 1) * P], src[:, b * P : (b + 1) * P], ident[:])
+            squared = keep.tile([P, 2 * W], F32, name="squared", bufs=PACK)
+            nc.scalar.activation(squared[:, :W], turned[:, :W], ACT.Square, scale=2.0)
+            nc.scalar.activation(squared[:, W:], turned[:, W:], ACT.Square)
+            both[t] = psum.tile([P, W], F32, name="both", tag=("high", "low")[t % 2], bufs=1)
+            for b in range(W // P):
+                for n in range(2):
+                    nc.tensor.matmul(
+                        both[t][:, b * P : (b + 1) * P], lhsT=squared[:, n * W + b * P : n * W + (b + 1) * P],
+                        rhs=ident[:], start=(n == 0), stop=(n == 1), is_transpose=True,
+                    )
 
         def put_root(t):
             nc.scalar.activation(ra[t][:], both[t][:], ACT.Sqrt, bias=quarter[:])
@@ -199,11 +212,11 @@ def tile_picked_pqlayksetpolar_none_p_kernel(tc, x_words, x_scales, d_words, d_s
 
         fetch(0)
         fetch(1)
-        squares(0)
         fetch(2)
-        put_root(0)
-        squares(1)
         fetch(3)
+        squares(0)
+        squares(1)
+        put_root(0)
         squares(2)
         put_root(1)
         squares(3)

from contextlib import ExitStack

import concourse.mybir as mybir
from concourse.masks import make_identity

F32 = mybir.dt.float32
BF16 = mybir.dt.bfloat16
I32 = mybir.dt.int32
U32 = mybir.dt.uint32
U16 = mybir.dt.uint16
U8 = mybir.dt.uint8
FP8X4 = mybir.dt.float8_e4m3fn_x4
ACT = mybir.ActivationFunctionType
ALU = mybir.AluOpType

P = 128
PACK = 4
TABLE = 2048
S = 512
W = 256
HALF = 256
FLOPS = 2 * 2 * 512 * 512 * 512


def tile_picked_pqlayksetpolar_none_p_kernel(tc, x_words, x_scales, d_words, d_scales, gn, w1, offs, k1, n1, n2, n3, n4, n5, out):
    nc = tc.nc
    with ExitStack() as ctx:
        lists = ctx.enter_context(tc.tile_pool(name="lists", bufs=1))
        keep = ctx.enter_context(tc.tile_pool(name="keep", bufs=1))
        psum = ctx.enter_context(tc.psum_pool(name="psum", bufs=1))

        def load_list(src, name):
            tile = lists.tile([P, src.shape[1]], U16, name=name)
            nc.sync.dma_start(tile[:], src)
            return tile

        def halves():
            return [slice(u * HALF, (u + 1) * HALF) for u in range(S // HALF)]

        def entries(tile, cols):
            return tile[:, cols.start // 16 : cols.stop // 16]

        d_bytes = keep.tile([P, TABLE], U8, name="d_bytes")
        x_bytes = keep.tile([P, TABLE], U8, name="x_bytes")
        nc.vector.memset(d_bytes[:].bitcast(I32), 0)
        nc.vector.memset(x_bytes[:].bitcast(I32), 0)

        k1_t = load_list(k1, "k1_t")
        nc.sync.dma_start(d_bytes[0:P:8, :].bitcast(I32), d_scales[0].bitcast(I32))
        offs_t = load_list(offs, "offs_t")
        nc.sync.dma_start(x_bytes[0:P:8, :].bitcast(I32), x_scales[0].bitcast(I32))
        d_table = keep.tile([P, TABLE], U32, name="d_table")
        nc.sync.dma_start(d_table[:].bitcast(I32), d_words[0].rearrange("p n t -> p (n t)").bitcast(I32))
        n2_t = load_list(n2, "n2_t")
        n1_t = load_list(n1, "n1_t")
        n3_t = load_list(n3, "n3_t")
        x_table = keep.tile([P, TABLE], U32, name="x_table")
        nc.sync.dma_start(x_table[:].bitcast(I32), x_words[0].rearrange("p n t -> p (n t)").bitcast(I32))
        n4_t = load_list(n4, "n4_t")
        n5_t = load_list(n5, "n5_t")
        gain = keep.tile([P, PACK], F32, name="gain")
        nc.gpsimd.dma_start(gain[:], gn.rearrange("(p t) o -> p (t o)", t=PACK))
        w_raw = [keep.tile([P, PACK, HALF], F32, name="w_raw%d" % u) for u in range(2)]
        for u, cols in enumerate(halves()):
            nc.sync.dma_start(w_raw[u][:], w1.rearrange("(p j) c -> p j c", j=PACK)[:, :, cols])
        sixteenth = keep.tile([P, 1], F32, name="sixteenth")
        nc.vector.memset(sixteenth[:], 0.0625)
        quarter = keep.tile([P, 1], F32, name="quarter")
        nc.scalar.activation(quarter[:], sixteenth[:], ACT.Sqrt)

        ident = keep.tile([P, P], F32, name="ident")
        make_identity(nc, ident[:])

        d_bytes_g = keep.tile([P, S], U8, name="d_bytes_g")
        nc.vector.tensor_copy(d_bytes_g[:], d_bytes[:].indirect(k1_t[:]))
        x_bytes_g = keep.tile([P, S], U8, name="x_bytes_g")
        nc.vector.tensor_copy(x_bytes_g[:], x_bytes[:].indirect(offs_t[:]))
        planes = keep.tile([P, 2 * S], U8, name="planes", align_bytes=64)
        d_plane = planes[:, :S]
        x_plane = planes[:, S:]
        nc.vector.tensor_copy(
            d_plane.rearrange("p (t c i) -> p c t i", t=PACK, i=16),
            d_bytes_g[:].rearrange("p (c i t) -> p c t i", t=PACK, i=16),
        )
        nc.vector.tensor_copy(x_plane.bitcast(U32), x_bytes_g[:].bitcast(U32))
        for s in range(1, 4):
            nc.scalar.dma_start(planes[s:P:32, :].bitcast(I32), planes[8 * s : P : 32, :].bitcast(I32))

        d_picked = keep.tile([P, S], U32, name="d_picked")
        nc.vector.tensor_copy(d_picked[:], d_table[:].indirect(k1_t[:]))
        d_codes = keep.tile([P, S], U32, name="d_codes", align_bytes=64)
        nc.vector.tensor_copy(
            d_codes[:].rearrange("p (t c i) -> p c t i", t=PACK, i=4),
            d_picked[:].rearrange("p (c i t) -> p c t i", t=PACK, i=4),
        )
        x_codes = keep.tile([P, S], U32, name="x_codes", align_bytes=64)
        for cols in halves():
            nc.vector.tensor_copy(x_codes[:, cols], x_table[:].indirect(entries(offs_t, cols)))

        gain16 = keep.tile([P, PACK], F32, name="gain16", tag="gain_then_far")
        nc.scalar.activation(gain16[:], gain[:], ACT.Copy, scale=0.0625)

        halves_of_s = halves()

        def product(codes, plane, t, moving, moving_plane, bank, bufs):
            rows = slice(t * P, (t + 1) * P)
            acc = psum.tile([P, moving.shape[1]], F32, name="acc", tag=bank, bufs=bufs)
            nc.tensor.matmul_mx(
                acc[:], lhsT=codes[:, rows].bitcast(FP8X4), lhsT_scale=plane[:, rows],
                rhs=moving.bitcast(FP8X4), rhs_scale=moving_plane, start=True, stop=True,
            )
            return acc

        ds = [keep.tile([P, S], F32, name="ds%d" % t) for t in range(PACK)]

        def first_layer(t):
            for cols in halves_of_s if t == 0 else [slice(0, S)]:
                acc = product(d_codes, d_plane, t, x_codes[:, cols], x_plane[:, cols], "first", 2)
                nc.scalar.activation(ds[t][:, cols], acc[:], ACT.Copy, scale=gain16[:, t : t + 1])
            nc.scalar.activation(pa[t][:], ds[t][:].indirect(n2_t[:]), ACT.Copy)

        w_grouped = keep.tile([P, PACK * 512], BF16, name="w_grouped", align_bytes=64)
        for u, copy in enumerate((nc.vector.tensor_copy, nc.vector.tensor_copy)):
            copy(
                w_grouped[:].rearrange("p (t m j) -> p m t j", t=PACK, j=PACK)[:, u * 64 : (u + 1) * 64],
                w_raw[u][:].rearrange("p j (m t) -> p m t j", t=PACK),
            )

        w_codes = keep.tile([P, 512], U32, name="w_codes", align_bytes=64)
        w_plane = keep.tile([P, 512], U8, name="w_plane", align_bytes=64)
        nc.vector.quantize_mx(w_codes[:].bitcast(FP8X4), w_plane[:], w_grouped[:])

        z_rows = [keep.tile([P, PACK, HALF], BF16, name="z_rows%d" % u) for u in range(2)]
        pa = [keep.tile([P, W], F32, name="pa%d" % t, tag="pa%d" % t, align_bytes=64) for t in range(PACK)]
        for t in range(PACK):
            first_layer(t)
            nc.vector.tensor_copy(ds[t][:].indirect(n1_t[:]), pa[t][:])

        h2 = [keep.tile([P, S], F32, name="h2_%d" % t) for t in range(PACK)]
        z_codes = keep.tile([P, S], U32, name="z_codes", align_bytes=64)
        z_plane = keep.tile([P, S], U8, name="z_plane", align_bytes=64)
        z_grouped = [keep.tile([P, PACK * HALF], BF16, name="z_grouped%d" % u, align_bytes=64) for u in range(2)]
        far = keep.tile([P, PACK, S], F32, name="far", tag="gain_then_far")

        def make_z(t, u):
            cols = halves_of_s[u]
            nc.scalar.activation(far[:, t, cols], ds[t][:].indirect(entries(n3_t, cols)), ACT.Copy, scale=-0.5)
            nc.vector.tensor_tensor(z_rows[u][:, t, :], ds[t][:, cols], far[:, t, cols], ALU.add)

        def group_z(u, copy):
            copy(
                z_grouped[u][:].rearrange("p (c i t) -> p c t i", t=PACK, i=4),
                z_rows[u][:].rearrange("p t (c i) -> p c t i", i=4),
            )

        def quantize_z(u):
            cols = halves_of_s[u]
            nc.vector.quantize_mx(z_codes[:, cols].bitcast(FP8X4), z_plane[:, cols], z_grouped[u][:])

        for t, u in ((0, 0), (1, 0), (0, 1), (2, 0), (1, 1), (3, 0), (2, 1), (3, 1)):
            make_z(t, u)
        group_z(0, nc.scalar.copy)
        group_z(1, nc.vector.tensor_copy)
        quantize_z(1)
        quantize_z(0)

        out_rows = out.rearrange("(p t) s -> p t s", t=PACK)
        res = [keep.tile([P, S], F32, name="res%d" % t) for t in range(PACK)]
        ra = [keep.tile([P, W], F32, name="ra%d" % t) for t in range(PACK)]
        a_half = [keep.tile([P, W], F32, name="a_half%d" % t) for t in range(PACK)]
        pb = [keep.tile([P, W], F32, name="pb%d" % t) for t in range(PACK)]
        both = {}

        def fetch(t):
            if t == 0:
                low, high = halves_of_s
                acc = product(w_codes, w_plane, t, z_codes[:, high], z_plane[:, high], "high", 1)
                nc.scalar.copy(h2[t][:, high], acc[:])
                acc = product(w_codes, w_plane, t, z_codes[:, low], z_plane[:, low], "low", 1)
                nc.vector.tensor_copy(h2[t][:, low], acc[:])
            else:
                acc = product(w_codes, w_plane, t, z_codes[:], z_plane[:], "rows%d" % t, 1)
                nc.scalar.copy(h2[t][:], acc[:])
            if t == 0:
                nc.vector.tensor_scalar(a_half[t][:], h2[t][:].indirect(n4_t[:]), -0.5, 0.0, ALU.mult, ALU.add)
                nc.vector.tensor_copy(pb[t][:], h2[t][:].indirect(n5_t[:]))
            else:
                nc.scalar.activation(a_half[t][:], h2[t][:].indirect(n4_t[:]), ACT.Copy, scale=-0.5)
                nc.scalar.activation(pb[t][:], h2[t][:].indirect(n5_t[:]), ACT.Copy)
            nc.vector.tensor_tensor(res[t][:].indirect(n5_t[:]), pb[t][:], a_half[t][:], ALU.add)

        def squares(t):
            turned = psum.tile([P, 2 * W], F32, name="turned", tag="first", bufs=2)
            for n, src in enumerate((a_half[t], pb[t])):
                for b in range(W // P):
                    nc.tensor.transpose(turned[:, n * W + b * P : n * W + (b + 1) * P], src[:, b * P : (b + 1) * P], ident[:])
            squared = keep.tile([P, 2 * W], F32, name="squared", bufs=PACK)
            nc.scalar.activation(squared[:, :W], turned[:, :W], ACT.Square, scale=2.0)
            nc.scalar.activation(squared[:, W:], turned[:, W:], ACT.Square)
            both[t] = psum.tile([P, W], F32, name="both", tag=("high", "low")[t % 2], bufs=1)
            for b in range(W // P):
                for n in range(2):
                    nc.tensor.matmul(
                        both[t][:, b * P : (b + 1) * P], lhsT=squared[:, n * W + b * P : n * W + (b + 1) * P],
                        rhs=ident[:], start=(n == 0), stop=(n == 1), is_transpose=True,
                    )

        def put_root(t):
            nc.scalar.activation(ra[t][:], both[t][:], ACT.Sqrt, bias=quarter[:])
            nc.vector.tensor_copy(res[t][:].indirect(n4_t[:]), ra[t][:])
            nc.sync.dma_start(out_rows[:, t, :], res[t][:])

        fetch(0)
        fetch(1)
        fetch(2)
        fetch(3)
        squares(0)
        squares(1)
        put_root(0)
        squares(2)
        put_root(1)
        squares(3)
        put_root(2)
        put_root(3)
